import numpy as np
import ml_dtypes


def mxq(x, axis, fmt="e4m3"):
    dtype, down = {"e4m3": (ml_dtypes.float8_e4m3fn, 7), "e5m2": (ml_dtypes.float8_e5m2, 14)}[fmt]
    v = np.moveaxis(np.asarray(x, np.float32).astype(ml_dtypes.bfloat16).astype(np.float64), axis, -1)
    blocks = v.reshape(v.shape[:-1] + (-1, 32))
    amax = np.abs(blocks).max(-1, keepdims=True)
    byte = np.maximum(np.where(amax > 0, np.frexp(amax)[1] - 1 + 127, 0) - down, 1)
    scale = np.exp2(byte - 127.0)
    codes = (blocks / scale).astype(np.float32).astype(dtype).astype(np.float64)
    return np.moveaxis((codes * scale).reshape(v.shape), -1, axis)


WIDE = False


def mx_kscale(k):
    if not WIDE:
        return np.ones(k)
    levels = np.array([10, -10, 5, -5, 0])
    if k % 512:
        return np.exp2(np.random.permutation(np.resize(levels, k // 32))).repeat(32)
    a = np.empty((k // 512, 16))
    for p in range(k // 512):
        a[p, :8] = np.random.permutation(np.resize(levels, 8))
        for g in range(8):
            far = levels[np.abs(levels - a[p, g]) >= 10]
            a[p, g + 8] = far[np.random.randint(len(far))]
    return np.exp2(a.ravel()).repeat(32)


def f64(x):
    return np.asarray(x).astype(np.float64)


def striped(idx):
    return np.tile(idx.reshape(-1, 16).T, (8, 1)).astype(np.uint16)


def unstriped(offs):
    return offs[:16].T.reshape(-1).astype(np.int64)


def striped8(idx):
    return np.concatenate([x.reshape(-1, 16).T for x in idx]).astype(np.uint16)


def runs(offs, k):
    lists = np.stack([offs[16 * r : 16 * r + 16].T.reshape(-1) for r in range(8)]).astype(np.int64)
    return lists[np.arange(k) % 512 // 64]


def pack_weight(w):
    k, n = w.shape
    w = f64(np.asarray(w, np.float32).astype(ml_dtypes.bfloat16)).reshape(k // 32, 32, n)
    amax = np.abs(w).max(1)
    byte = np.clip(np.where(amax > 0, np.frexp(amax)[1] - 1 + 127 - 7, 1), 1, 254)
    scaled = (w * np.exp2(127.0 - byte)[:, None, :]).reshape(k, n).astype(np.float32)
    words = np.ascontiguousarray(scaled.reshape(k // 512, 128, 4, n).transpose(0, 1, 3, 2)).astype(ml_dtypes.float8_e4m3fn).view(np.uint8)
    return words, np.ascontiguousarray(byte.astype(np.uint8).reshape(k // 512, 16, n))


def unpack_weight(words, scales):
    g, p, n, _ = words.shape
    vals = np.ascontiguousarray(words).view(ml_dtypes.float8_e4m3fn).astype(np.float64) * np.repeat(np.exp2(scales.astype(np.float64) - 127.0), 8, axis=1)[..., None]
    return vals.transpose(0, 1, 3, 2).reshape(g * 512, n)


K, T, S, H, G, U = 512, 2048, 256, 512, 2048, 1024


def setup_inputs():
    n = np.random.standard_normal
    s = mx_kscale(K)[:, None]
    packed_xT = pack_weight(n((K, T)) * s)
    packed_dT = pack_weight(n((K, G)) / s)
    return {
        "x_words": packed_xT[0],
        "x_scales": packed_xT[1],
        "w1": (n((K, H)) / np.sqrt(K) / s).astype(np.float32),
        "gs": (np.random.uniform(0.5, 1.5, (K, 1)) * s).astype(np.float32),
        "d_words": packed_dT[0],
        "d_scales": packed_dT[1],
        "offs": striped(np.random.permutation(T)[:S]),
        "n1": striped8(np.stack([np.random.permutation(S) for _ in range(8)])),
        "n2": striped8(np.stack([np.random.permutation(S) for _ in range(8)])),
        "ka": striped8(np.random.randint(0, G, (8, H))),
        "kb": striped8(np.random.randint(0, G, (8, H))),
        "n3": striped(np.random.permutation(U)[:S]),
        "n4": striped(np.random.permutation(S)),
    }


def reference(x_words, x_scales, w1, gs, d_words, d_scales, offs, n1, n2, ka, kb, n3, n4):
    d_ka = unpack_weight(d_words, d_scales)[np.arange(K)[:, None], runs(ka, K)]
    xq = unpack_weight(x_words, x_scales)[:, unstriped(offs)]
    y = mxq(f64(w1), 0, "e4m3").T @ xq
    z = f64(gs) * (y * (y[np.arange(H)[:, None], runs(n1, H)] - (y[np.arange(H)[:, None], runs(n2, H)])))
    zq = mxq(z, 0, "e4m3")
    d_kb = unpack_weight(d_words, d_scales)[np.arange(K)[:, None], runs(kb, K)]
    h = 0.0625 * (d_ka.T @ zq + d_kb.T @ zq)
    nw = np.maximum(h, h[:, unstriped(n4)])
    out = np.zeros((H, U))
    out[:, unstriped(n3)] = nw
    return out

@@ -1,0 +1,215 @@
+from contextlib import ExitStack
+
+import concourse.mybir as mybir
+
+K, T, S, H, G, U = 512, 2048, 256, 512, 2048, 1024
+FLOPS = 3 * 2 * K * H * S
+
+F32 = mybir.dt.float32
+BF16 = mybir.dt.bfloat16
+I32 = mybir.dt.int32
+U32 = mybir.dt.uint32
+U16 = mybir.dt.uint16
+U8 = mybir.dt.uint8
+FP8X4 = mybir.dt.float8_e4m3fn_x4
+COPY = mybir.ActivationFunctionType.Copy
+ALU = mybir.AluOpType
+
+P = 128
+PACK = 4
+HALF = S // 2
+Y_WINDOW = 2 * S
+H_WINDOW = S + 16
+PAGES = 3
+
+
+def tile_picked_daqwindpags_none_p_kernel(
+    tc, x_words, x_scales, w1, gs, d_words, d_scales, offs, n1, n2, ka, kb, n3, n4, out
+):
+    nc = tc.nc
+    with ExitStack() as ctx:
+        keep = ctx.enter_context(tc.tile_pool(name="keep", bufs=1))
+        psum = ctx.enter_context(tc.psum_pool(name="psum", bufs=1))
+
+        def load_list(name, src):
+            tile = keep.tile(list(src.shape), U16, name=name)
+            nc.sync.dma_start(tile[:], src)
+            return tile
+
+        def as_words(src):
+            return src[0].rearrange("p n r -> p (n r)").bitcast(I32)
+
+        y_win = [keep.tile([P, Y_WINDOW], F32, name="y_win%d" % t) for t in range(PACK)]
+        h_win = [keep.tile([P, H_WINDOW], F32, name="h_win%d" % m) for m in range(H // P)]
+        d_scale_table = keep.tile([P, G], U8, name="d_scale_table")
+        x_scale_table = keep.tile([P, T], U8, name="x_scale_table")
+
+        nc.vector.memset(h_win[0][:, S:], 0.0)
+        for m in range(1, H // P):
+            nc.scalar.activation(h_win[m][:, S:], h_win[0][:, S:], COPY)
+        nc.vector.memset(d_scale_table[:].bitcast(I32), 0)
+        nc.vector.memset(x_scale_table[:].bitcast(I32), 0)
+
+        ka_sb = load_list("ka_sb", ka)
+        kb_sb = load_list("kb_sb", kb)
+        nc.sync.dma_start(d_scale_table[0:P:8, :].bitcast(I32), d_scales[0].bitcast(I32))
+        for c in range(4):
+            nc.scalar.dma_start(x_scale_table[c:P:32, :].bitcast(I32), x_scales[0, c:16:4, :].bitcast(I32))
+
+        w_rows = w1.rearrange("(p j) c -> p j c", j=PACK)
+        w_raw = [keep.tile([P, PACK, H // 2], F32, name="w_raw%d" % u, tag="w_raw%d" % u) for u in range(2)]
+        for u in range(2):
+            nc.sync.dma_start(w_raw[u][:], w_rows[:, :, u * (H // 2) : (u + 1) * (H // 2)])
+        offs_sb = load_list("offs_sb", offs)
+        x_table = keep.tile([P, T], U32, name="x_table")
+        nc.sync.dma_start(x_table[:].bitcast(I32), as_words(x_words))
+        n1_sb = load_list("n1_sb", n1)
+        n2_sb = load_list("n2_sb", n2)
+        d_table = keep.tile([P, G], U32, name="d_table", tag="d_table")
+        nc.sync.dma_start(d_table[:].bitcast(I32), as_words(d_words))
+        gs_sb = keep.tile([P, PACK], F32, name="gs_sb")
+        nc.sync.dma_start(gs_sb[:], gs.rearrange("(p t) o -> p (t o)", t=PACK))
+        n4_sb = load_list("n4_sb", n4)
+        n3_sb = load_list("n3_sb", n3)
+
+        d_scale_plane = keep.tile([P, 2 * H], U8, name="d_scale_plane", align_bytes=64)
+        nc.vector.memset(d_scale_plane[:].bitcast(I32), 0)
+        for t in range(PACK):
+            nc.vector.memset(y_win[t][:, S:], 0.0)
+        pages = [keep.tile([P, U], F32, name="page0")]
+        nc.vector.memset(pages[0][:], 0.0)
+
+        d_scale_picked = keep.tile([P, 2 * H], U8, name="d_scale_picked")
+        nc.vector.tensor_copy(d_scale_picked[:, :H], d_scale_table[:].indirect(ka_sb[:]))
+        nc.vector.tensor_copy(d_scale_picked[:, H:], d_scale_table[:].indirect(kb_sb[:]))
+        x_scale_picked = keep.tile([P, S], U8, name="x_scale_picked", align_bytes=64)
+        nc.vector.tensor_copy(x_scale_picked[:], x_scale_table[:].indirect(offs_sb[:]))
+        for c in range(4):
+            nc.sync.dma_start(d_scale_plane[c:P:32, :].bitcast(I32), d_scale_picked[8 * c : P : 32, :].bitcast(I32))
+
+        w_bf = keep.tile([P, PACK, P, PACK], BF16, name="w_bf", align_bytes=64)
+        for u in range(2):
+            nc.scalar.activation(
+                w_bf[:, :, u * (P // 2) : (u + 1) * (P // 2), :].rearrange("p t m j -> p m j t"),
+                w_raw[u][:].rearrange("p j (m t) -> p m j t", t=PACK),
+                COPY,
+            )
+        pages.append(keep.tile([P, U], F32, name="page1", tag="w_raw1"))
+        nc.scalar.activation(pages[1][:], pages[0][:], COPY)
+        w_codes = keep.tile([P, PACK, P], U32, name="w_codes", align_bytes=64)
+        w_scale = keep.tile([P, PACK, P], U8, name="w_scale", align_bytes=64)
+        for t in range(PACK):
+            nc.vector.quantize_mx(
+                out=w_codes[:, t, :].bitcast(FP8X4),
+                scales=w_scale[:, t, :],
+                in_=w_bf[:, t, :, :].rearrange("p m j -> p (m j)"),
+            )
+
+        x_picked = keep.tile([P, S], U32, name="x_picked", align_bytes=64)
+        nc.vector.tensor_copy(x_picked[:], x_table[:].indirect(offs_sb[:]))
+
+        for t in range(PACK):
+            y_ps = psum.tile([P, S], F32, name="y_ps%d" % t)
+            nc.tensor.matmul_mx(
+                out=y_ps[:],
+                lhsT=w_codes[:, t, :].bitcast(FP8X4),
+                lhsT_scale=w_scale[:, t, :],
+                rhs=x_picked[:].bitcast(FP8X4),
+                rhs_scale=x_scale_picked[:],
+                start=True,
+                stop=True,
+            )
+            if t == 0:
+                nc.scalar.activation(y_win[t][:, :S], y_ps[:], COPY)
+            else:
+                nc.vector.tensor_copy(y_win[t][:, :S], y_ps[:])
+
+        d_picked = {}
+
+        def pick_codewords(name, u, tag):
+            codes = {"a": ka_sb, "b": kb_sb}[name]
+            tile = keep.tile([P, H // 2], U32, name="d_picked_%s%d" % (name, u), tag=tag, align_bytes=64)
+            nc.vector.tensor_copy(tile[:], d_table[:].indirect(codes[:, 16 * u : 16 * (u + 1)]))
+            d_picked[name, u] = tile
+
+        pick_codewords("a", 0, "d_picked_a0")
+        pick_codewords("b", 0, "d_picked_b0")
+
+        z_codes = keep.tile([P, S], U32, name="z_codes", align_bytes=64)
+        z_scale = keep.tile([P, S], U8, name="z_scale", align_bytes=64)
+        h_ps = [psum.tile([P, S], F32, name="h_ps%d" % m) for m in range(H // P)]
+
+        def second_product(m, cols):
+            for i, name in enumerate(("a", "b")):
+                nc.tensor.matmul_mx(
+                    out=h_ps[m][:, cols],
+                    lhsT=d_picked[name, m // 2][:, (m % 2) * P : (m % 2 + 1) * P].bitcast(FP8X4),
+                    lhsT_scale=d_scale_plane[:, i * H + m * P : i * H + (m + 1) * P],
+                    rhs=z_codes[:, cols].bitcast(FP8X4),
+                    rhs_scale=z_scale[:, cols],
+                    start=(i == 0),
+                    stop=(i == 1),
+                )
+
+        for half in range(2):
+            cols = slice(half * HALF, (half + 1) * HALF)
+            entries = slice(half * HALF // 16, (half + 1) * HALF // 16)
+            y_n1 = keep.tile([P, PACK, HALF], F32, name="y_n1_%d" % half)
+            y_n2 = keep.tile([P, PACK, HALF], F32, name="y_n2_%d" % half)
+            diff = keep.tile([P, PACK, HALF], F32, name="diff%d" % half)
+            z = keep.tile([P, PACK, HALF], F32, name="z%d" % half)
+            for t in range(PACK):
+                nc.scalar.activation(y_n1[:, t, :], y_win[t][:].indirect(n1_sb[:, entries]), COPY)
+                nc.scalar.activation(y_n2[:, t, :], y_win[t][:].indirect(n2_sb[:, entries]), COPY)
+                nc.vector.tensor_tensor(diff[:, t, :], y_n1[:, t, :], y_n2[:, t, :], ALU.subtract)
+                nc.vector.scalar_tensor_tensor(
+                    z[:, t, :], diff[:, t, :], gs_sb[:, t : t + 1], y_win[t][:, cols], ALU.mult, ALU.mult
+                )
+            z_bf = keep.tile([P, HALF, PACK], BF16, name="z_bf%d" % half, tag="z_bf%d" % half, align_bytes=64)
+            nc.vector.tensor_copy(
+                z_bf[:].rearrange("p (c i) t -> p c t i", i=4),
+                z[:].rearrange("p t (c i) -> p c t i", i=4),
+            )
+            nc.vector.quantize_mx(
+                out=z_codes[:, cols].bitcast(FP8X4),
+                scales=z_scale[:, cols],
+                in_=z_bf[:].rearrange("p c t -> p (c t)"),
+            )
+            if half == 0:
+                second_product(0, cols)
+                nc.vector.tensor_scalar(h_win[0][:, cols], h_ps[0][:, cols], 0.0625, None, ALU.mult)
+            else:
+                second_product(0, cols)
+                nc.scalar.activation(h_win[0][:, cols], h_ps[0][:, cols], COPY, scale=0.0625)
+
+        nw = [keep.tile([P, S], F32, name="nw%d" % m) for m in range(H // P)]
+
+        def product_out(m):
+            second_product(m, slice(0, S))
+            nc.vector.tensor_scalar(h_win[m][:, :S], h_ps[m][:], 0.0625, None, ALU.mult)
+
+        def larger(m):
+            h_n4 = keep.tile([P, S], F32, name="h_n4_%d" % m, tag="h_n4_%d" % m, align_bytes=64)
+            nc.scalar.activation(h_n4[:], h_win[m][:].indirect(n4_sb[:]), COPY)
+            nc.vector.tensor_tensor(nw[m][:], h_n4[:], h_win[m][:, :S], ALU.max)
+
+        def put(m):
+            page = pages[m % PAGES]
+            nc.scalar.activation(page[:].indirect(n3_sb[:]), nw[m][:], COPY)
+            nc.sync.dma_start(out[m * P : (m + 1) * P, :], page[:])
+
+        product_out(1)
+        pick_codewords("a", 1, "z_bf1")
+        larger(0)
+        pick_codewords("b", 1, "h_n4_0")
+        larger(1)
+        product_out(2)
+        product_out(3)
+        pages.append(keep.tile([P, U], F32, name="page2", tag="d_table"))
+        nc.vector.memset(pages[2][:], 0.0)
+        put(0)
+        larger(2)
+        put(1)
+        larger(3)
+        put(2)
+        put(3)

@@ -44,48 +44,41 @@ def tile_picked_daqwindpags_none_p_kernel(
         d_scale_table = keep.tile([P, G], U8, name="d_scale_table")
         x_scale_table = keep.tile([P, T], U8, name="x_scale_table")
 
-        nc.vector.memset(h_win[0][:, S:], 0.0)
-        for m in range(1, H // P):
-            nc.scalar.activation(h_win[m][:, S:], h_win[0][:, S:], COPY)
-        nc.vector.memset(d_scale_table[:].bitcast(I32), 0)
         nc.vector.memset(x_scale_table[:].bitcast(I32), 0)
+        nc.gpsimd.memset(d_scale_table[:].bitcast(I32), 0)
 
         ka_sb = load_list("ka_sb", ka)
         kb_sb = load_list("kb_sb", kb)
         nc.sync.dma_start(d_scale_table[0:P:8, :].bitcast(I32), d_scales[0].bitcast(I32))
         for c in range(4):
-            nc.scalar.dma_start(x_scale_table[c:P:32, :].bitcast(I32), x_scales[0, c:16:4, :].bitcast(I32))
+            queue = nc.sync if c >= 2 else nc.scalar
+            queue.dma_start(x_scale_table[c:P:32, :].bitcast(I32), x_scales[0, c:16:4, :].bitcast(I32))
 
         w_rows = w1.rearrange("(p j) c -> p j c", j=PACK)
         w_raw = [keep.tile([P, PACK, H // 2], F32, name="w_raw%d" % u, tag="w_raw%d" % u) for u in range(2)]
         for u in range(2):
             nc.sync.dma_start(w_raw[u][:], w_rows[:, :, u * (H // 2) : (u + 1) * (H // 2)])
         offs_sb = load_list("offs_sb", offs)
-        x_table = keep.tile([P, T], U32, name="x_table")
-        nc.sync.dma_start(x_table[:].bitcast(I32), as_words(x_words))
         n1_sb = load_list("n1_sb", n1)
         n2_sb = load_list("n2_sb", n2)
-        d_table = keep.tile([P, G], U32, name="d_table", tag="d_table")
-        nc.sync.dma_start(d_table[:].bitcast(I32), as_words(d_words))
-        gs_sb = keep.tile([P, PACK], F32, name="gs_sb")
-        nc.sync.dma_start(gs_sb[:], gs.rearrange("(p t) o -> p (t o)", t=PACK))
-        n4_sb = load_list("n4_sb", n4)
-        n3_sb = load_list("n3_sb", n3)
+        x_table = keep.tile([P, T], U32, name="x_table")
+        nc.sync.dma_start(x_table[:].bitcast(I32), as_words(x_words))
 
         d_scale_plane = keep.tile([P, 2 * H], U8, name="d_scale_plane", align_bytes=64)
         nc.vector.memset(d_scale_plane[:].bitcast(I32), 0)
         for t in range(PACK):
-            nc.vector.memset(y_win[t][:, S:], 0.0)
-        pages = [keep.tile([P, U], F32, name="page0")]
-        nc.vector.memset(pages[0][:], 0.0)
+            nc.gpsimd.memset(y_win[t][:, S:], 0.0)
+        for m in range(H // P):
+            nc.vector.memset(h_win[m][:, S:], 0.0)
+        pages = [keep.tile([P, U], F32, name="page%d" % i) for i in range(PAGES)]
+        for page in pages:
+            nc.gpsimd.memset(page[:], 0.0)
 
         d_scale_picked = keep.tile([P, 2 * H], U8, name="d_scale_picked")
         nc.vector.tensor_copy(d_scale_picked[:, :H], d_scale_table[:].indirect(ka_sb[:]))
         nc.vector.tensor_copy(d_scale_picked[:, H:], d_scale_table[:].indirect(kb_sb[:]))
         x_scale_picked = keep.tile([P, S], U8, name="x_scale_picked", align_bytes=64)
         nc.vector.tensor_copy(x_scale_picked[:], x_scale_table[:].indirect(offs_sb[:]))
-        for c in range(4):
-            nc.sync.dma_start(d_scale_plane[c:P:32, :].bitcast(I32), d_scale_picked[8 * c : P : 32, :].bitcast(I32))
 
         w_bf = keep.tile([P, PACK, P, PACK], BF16, name="w_bf", align_bytes=64)
         for u in range(2):
@@ -94,8 +87,15 @@ def tile_picked_daqwindpags_none_p_kernel(
                 w_raw[u][:].rearrange("p j (m t) -> p m j t", t=PACK),
                 COPY,
             )
-        pages.append(keep.tile([P, U], F32, name="page1", tag="w_raw1"))
-        nc.scalar.activation(pages[1][:], pages[0][:], COPY)
+        gs_sb = keep.tile([P, PACK], F32, name="gs_sb", tag="w_raw0")
+        nc.scalar.dma_start(gs_sb[:], gs.rearrange("(p t) o -> p (t o)", t=PACK))
+        d_table = keep.tile([P, G], U32, name="d_table", tag="w_raw1")
+        for queue, cols in ((nc.sync, slice(0, G // 2)), (nc.scalar, slice(G // 2, G))):
+            queue.dma_start(d_table[:, cols].bitcast(I32), as_words(d_words)[:, cols])
+        n4_sb = load_list("n4_sb", n4)
+        n3_sb = load_list("n3_sb", n3)
+        for c in range(4):
+            nc.sync.dma_start(d_scale_plane[c:P:32, :].bitcast(I32), d_scale_picked[8 * c : P : 32, :].bitcast(I32))
         w_codes = keep.tile([P, PACK, P], U32, name="w_codes", align_bytes=64)
         w_scale = keep.tile([P, PACK, P], U8, name="w_scale", align_bytes=64)
         for t in range(PACK):
@@ -156,31 +156,34 @@ def tile_picked_daqwindpags_none_p_kernel(
             entries = slice(half * HALF // 16, (half + 1) * HALF // 16)
             y_n1 = keep.tile([P, PACK, HALF], F32, name="y_n1_%d" % half)
             y_n2 = keep.tile([P, PACK, HALF], F32, name="y_n2_%d" % half)
-            diff = keep.tile([P, PACK, HALF], F32, name="diff%d" % half)
-            z = keep.tile([P, PACK, HALF], F32, name="z%d" % half)
+            diff = keep.tile([P, PACK, HALF], F32, name="diff%d" % half, tag=("diff0", "z_bf0")[half], align_bytes=64)
+            z = keep.tile([P, PACK - half, HALF], F32, name="z%d" % half)
+            z_bf = keep.tile([P, HALF, PACK], BF16, name="z_bf%d" % half, tag="z_bf%d" % half, align_bytes=64)
+            staged = PACK - half
             for t in range(PACK):
                 nc.scalar.activation(y_n1[:, t, :], y_win[t][:].indirect(n1_sb[:, entries]), COPY)
                 nc.scalar.activation(y_n2[:, t, :], y_win[t][:].indirect(n2_sb[:, entries]), COPY)
                 nc.vector.tensor_tensor(diff[:, t, :], y_n1[:, t, :], y_n2[:, t, :], ALU.subtract)
                 nc.vector.scalar_tensor_tensor(
-                    z[:, t, :], diff[:, t, :], gs_sb[:, t : t + 1], y_win[t][:, cols], ALU.mult, ALU.mult
+                    z[:, t, :] if t < staged else z_bf[:, :, t],
+                    diff[:, t, :],
+                    gs_sb[:, t : t + 1],
+                    y_win[t][:, cols],
+                    ALU.mult,
+                    ALU.mult,
                 )
-            z_bf = keep.tile([P, HALF, PACK], BF16, name="z_bf%d" % half, tag="z_bf%d" % half, align_bytes=64)
-            nc.vector.tensor_copy(
-                z_bf[:].rearrange("p (c i) t -> p c t i", i=4),
-                z[:].rearrange("p t (c i) -> p c t i", i=4),
-            )
+                if t == staged - 1:
+                    nc.vector.tensor_copy(
+                        z_bf[:, :, :staged].rearrange("p (c i) t -> p c t i", i=4),
+                        z[:].rearrange("p t (c i) -> p c t i", i=4),
+                    )
             nc.vector.quantize_mx(
                 out=z_codes[:, cols].bitcast(FP8X4),
                 scales=z_scale[:, cols],
                 in_=z_bf[:].rearrange("p c t -> p (c t)"),
             )
-            if half == 0:
-                second_product(0, cols)
-                nc.vector.tensor_scalar(h_win[0][:, cols], h_ps[0][:, cols], 0.0625, None, ALU.mult)
-            else:
-                second_product(0, cols)
-                nc.scalar.activation(h_win[0][:, cols], h_ps[0][:, cols], COPY, scale=0.0625)
+            second_product(0, cols)
+            nc.scalar.activation(h_win[0][:, cols], h_ps[0][:, cols], COPY, scale=0.0625)
 
         nw = [keep.tile([P, S], F32, name="nw%d" % m) for m in range(H // P)]
 
@@ -205,8 +208,6 @@ def tile_picked_daqwindpags_none_p_kernel(
         larger(1)
         product_out(2)
         product_out(3)
-        pages.append(keep.tile([P, U], F32, name="page2", tag="d_table"))
-        nc.vector.memset(pages[2][:], 0.0)
         put(0)
         larger(2)
         put(1)

@@ -45,7 +45,10 @@ def tile_picked_daqwindpags_none_p_kernel(
         x_scale_table = keep.tile([P, T], U8, name="x_scale_table")
 
         nc.vector.memset(x_scale_table[:].bitcast(I32), 0)
-        nc.gpsimd.memset(d_scale_table[:].bitcast(I32), 0)
+        nc.vector.memset(d_scale_table[:].bitcast(I32), 0)
+        pages = [keep.tile([P, U], F32, name="page%d" % i) for i in range(2)]
+        nc.vector.memset(pages[0][:], 0.0)
+        nc.scalar.activation(pages[1][:], pages[0][:], COPY)
 
         ka_sb = load_list("ka_sb", ka)
         kb_sb = load_list("kb_sb", kb)
@@ -67,12 +70,9 @@ def tile_picked_daqwindpags_none_p_kernel(
         d_scale_plane = keep.tile([P, 2 * H], U8, name="d_scale_plane", align_bytes=64)
         nc.vector.memset(d_scale_plane[:].bitcast(I32), 0)
         for t in range(PACK):
-            nc.gpsimd.memset(y_win[t][:, S:], 0.0)
+            nc.vector.memset(y_win[t][:, S:], 0.0)
         for m in range(H // P):
             nc.vector.memset(h_win[m][:, S:], 0.0)
-        pages = [keep.tile([P, U], F32, name="page%d" % i) for i in range(PAGES)]
-        for page in pages:
-            nc.gpsimd.memset(page[:], 0.0)
 
         d_scale_picked = keep.tile([P, 2 * H], U8, name="d_scale_picked")
         nc.vector.tensor_copy(d_scale_picked[:, :H], d_scale_table[:].indirect(ka_sb[:]))
@@ -80,7 +80,7 @@ def tile_picked_daqwindpags_none_p_kernel(
         x_scale_picked = keep.tile([P, S], U8, name="x_scale_picked", align_bytes=64)
         nc.vector.tensor_copy(x_scale_picked[:], x_scale_table[:].indirect(offs_sb[:]))
 
-        w_bf = keep.tile([P, PACK, P, PACK], BF16, name="w_bf", align_bytes=64)
+        w_bf = keep.tile([P, PACK, P, PACK], BF16, name="w_bf", tag="w_bf", align_bytes=64)
         for u in range(2):
             nc.scalar.activation(
                 w_bf[:, :, u * (P // 2) : (u + 1) * (P // 2), :].rearrange("p t m j -> p m j t"),
@@ -104,6 +104,9 @@ def tile_picked_daqwindpags_none_p_kernel(
                 scales=w_scale[:, t, :],
                 in_=w_bf[:, t, :, :].rearrange("p m j -> p (m j)"),
             )
+
+        pages.append(keep.tile([P, U], F32, name="page2", tag="w_bf", align_bytes=64))
+        nc.scalar.activation(pages[2][:], pages[0][:], COPY)
 
         x_picked = keep.tile([P, S], U32, name="x_picked", align_bytes=64)
         nc.vector.tensor_copy(x_picked[:], x_table[:].indirect(offs_sb[:]))

from contextlib import ExitStack

import concourse.mybir as mybir

K, T, S, H, G, U = 512, 2048, 256, 512, 2048, 1024
FLOPS = 3 * 2 * K * H * S

F32 = mybir.dt.float32
BF16 = mybir.dt.bfloat16
I32 = mybir.dt.int32
U32 = mybir.dt.uint32
U16 = mybir.dt.uint16
U8 = mybir.dt.uint8
FP8X4 = mybir.dt.float8_e4m3fn_x4
COPY = mybir.ActivationFunctionType.Copy
ALU = mybir.AluOpType

P = 128
PACK = 4
HALF = S // 2
Y_WINDOW = 2 * S
H_WINDOW = S + 16
PAGES = 3


def tile_picked_daqwindpags_none_p_kernel(
    tc, x_words, x_scales, w1, gs, d_words, d_scales, offs, n1, n2, ka, kb, n3, n4, out
):
    nc = tc.nc
    with ExitStack() as ctx:
        keep = ctx.enter_context(tc.tile_pool(name="keep", bufs=1))
        psum = ctx.enter_context(tc.psum_pool(name="psum", bufs=1))

        def load_list(name, src):
            tile = keep.tile(list(src.shape), U16, name=name)
            nc.sync.dma_start(tile[:], src)
            return tile

        def as_words(src):
            return src[0].rearrange("p n r -> p (n r)").bitcast(I32)

        y_win = [keep.tile([P, Y_WINDOW], F32, name="y_win%d" % t) for t in range(PACK)]
        h_win = [keep.tile([P, H_WINDOW], F32, name="h_win%d" % m) for m in range(H // P)]
        d_scale_table = keep.tile([P, G], U8, name="d_scale_table")
        x_scale_table = keep.tile([P, T], U8, name="x_scale_table")

        nc.vector.memset(x_scale_table[:].bitcast(I32), 0)
        nc.vector.memset(d_scale_table[:].bitcast(I32), 0)
        pages = [keep.tile([P, U], F32, name="page%d" % i) for i in range(2)]
        nc.vector.memset(pages[0][:], 0.0)
        nc.scalar.activation(pages[1][:], pages[0][:], COPY)

        ka_sb = load_list("ka_sb", ka)
        kb_sb = load_list("kb_sb", kb)
        nc.sync.dma_start(d_scale_table[0:P:8, :].bitcast(I32), d_scales[0].bitcast(I32))
        for c in range(4):
            queue = nc.sync if c >= 2 else nc.scalar
            queue.dma_start(x_scale_table[c:P:32, :].bitcast(I32), x_scales[0, c:16:4, :].bitcast(I32))

        w_rows = w1.rearrange("(p j) c -> p j c", j=PACK)
        w_raw = [keep.tile([P, PACK, H // 2], F32, name="w_raw%d" % u, tag="w_raw%d" % u) for u in range(2)]
        for u in range(2):
            nc.sync.dma_start(w_raw[u][:], w_rows[:, :, u * (H // 2) : (u + 1) * (H // 2)])
        offs_sb = load_list("offs_sb", offs)
        n1_sb = load_list("n1_sb", n1)
        n2_sb = load_list("n2_sb", n2)
        x_table = keep.tile([P, T], U32, name="x_table")
        nc.sync.dma_start(x_table[:].bitcast(I32), as_words(x_words))

        d_scale_plane = keep.tile([P, 2 * H], U8, name="d_scale_plane", align_bytes=64)
        nc.vector.memset(d_scale_plane[:].bitcast(I32), 0)
        for t in range(PACK):
            nc.vector.memset(y_win[t][:, S:], 0.0)
        for m in range(H // P):
            nc.vector.memset(h_win[m][:, S:], 0.0)

        d_scale_picked = keep.tile([P, 2 * H], U8, name="d_scale_picked")
        nc.vector.tensor_copy(d_scale_picked[:, :H], d_scale_table[:].indirect(ka_sb[:]))
        nc.vector.tensor_copy(d_scale_picked[:, H:], d_scale_table[:].indirect(kb_sb[:]))
        x_scale_picked = keep.tile([P, S], U8, name="x_scale_picked", align_bytes=64)
        nc.vector.tensor_copy(x_scale_picked[:], x_scale_table[:].indirect(offs_sb[:]))

        w_bf = keep.tile([P, PACK, P, PACK], BF16, name="w_bf", tag="w_bf", align_bytes=64)
        for u in range(2):
            nc.scalar.activation(
                w_bf[:, :, u * (P // 2) : (u + 1) * (P // 2), :].rearrange("p t m j -> p m j t"),
                w_raw[u][:].rearrange("p j (m t) -> p m j t", t=PACK),
                COPY,
            )
        gs_sb = keep.tile([P, PACK], F32, name="gs_sb", tag="w_raw0")
        nc.scalar.dma_start(gs_sb[:], gs.rearrange("(p t) o -> p (t o)", t=PACK))
        d_table = keep.tile([P, G], U32, name="d_table", tag="w_raw1")
        for queue, cols in ((nc.sync, slice(0, G // 2)), (nc.scalar, slice(G // 2, G))):
            queue.dma_start(d_table[:, cols].bitcast(I32), as_words(d_words)[:, cols])
        n4_sb = load_list("n4_sb", n4)
        n3_sb = load_list("n3_sb", n3)
        for c in range(4):
            nc.sync.dma_start(d_scale_plane[c:P:32, :].bitcast(I32), d_scale_picked[8 * c : P : 32, :].bitcast(I32))
        w_codes = keep.tile([P, PACK, P], U32, name="w_codes", align_bytes=64)
        w_scale = keep.tile([P, PACK, P], U8, name="w_scale", align_bytes=64)
        for t in range(PACK):
            nc.vector.quantize_mx(
                out=w_codes[:, t, :].bitcast(FP8X4),
                scales=w_scale[:, t, :],
                in_=w_bf[:, t, :, :].rearrange("p m j -> p (m j)"),
            )

        pages.append(keep.tile([P, U], F32, name="page2", tag="w_bf", align_bytes=64))
        nc.scalar.activation(pages[2][:], pages[0][:], COPY)

        x_picked = keep.tile([P, S], U32, name="x_picked", align_bytes=64)
        nc.vector.tensor_copy(x_picked[:], x_table[:].indirect(offs_sb[:]))

        for t in range(PACK):
            y_ps = psum.tile([P, S], F32, name="y_ps%d" % t)
            nc.tensor.matmul_mx(
                out=y_ps[:],
                lhsT=w_codes[:, t, :].bitcast(FP8X4),
                lhsT_scale=w_scale[:, t, :],
                rhs=x_picked[:].bitcast(FP8X4),
                rhs_scale=x_scale_picked[:],
                start=True,
                stop=True,
            )
            if t == 0:
                nc.scalar.activation(y_win[t][:, :S], y_ps[:], COPY)
            else:
                nc.vector.tensor_copy(y_win[t][:, :S], y_ps[:])

        d_picked = {}

        def pick_codewords(name, u, tag):
            codes = {"a": ka_sb, "b": kb_sb}[name]
            tile = keep.tile([P, H // 2], U32, name="d_picked_%s%d" % (name, u), tag=tag, align_bytes=64)
            nc.vector.tensor_copy(tile[:], d_table[:].indirect(codes[:, 16 * u : 16 * (u + 1)]))
            d_picked[name, u] = tile

        pick_codewords("a", 0, "d_picked_a0")
        pick_codewords("b", 0, "d_picked_b0")

        z_codes = keep.tile([P, S], U32, name="z_codes", align_bytes=64)
        z_scale = keep.tile([P, S], U8, name="z_scale", align_bytes=64)
        h_ps = [psum.tile([P, S], F32, name="h_ps%d" % m) for m in range(H // P)]

        def second_product(m, cols):
            for i, name in enumerate(("a", "b")):
                nc.tensor.matmul_mx(
                    out=h_ps[m][:, cols],
                    lhsT=d_picked[name, m // 2][:, (m % 2) * P : (m % 2 + 1) * P].bitcast(FP8X4),
                    lhsT_scale=d_scale_plane[:, i * H + m * P : i * H + (m + 1) * P],
                    rhs=z_codes[:, cols].bitcast(FP8X4),
                    rhs_scale=z_scale[:, cols],
                    start=(i == 0),
                    stop=(i == 1),
                )

        for half in range(2):
            cols = slice(half * HALF, (half + 1) * HALF)
            entries = slice(half * HALF // 16, (half + 1) * HALF // 16)
            y_n1 = keep.tile([P, PACK, HALF], F32, name="y_n1_%d" % half)
            y_n2 = keep.tile([P, PACK, HALF], F32, name="y_n2_%d" % half)
            diff = keep.tile([P, PACK, HALF], F32, name="diff%d" % half, tag=("diff0", "z_bf0")[half], align_bytes=64)
            z = keep.tile([P, PACK - half, HALF], F32, name="z%d" % half)
            z_bf = keep.tile([P, HALF, PACK], BF16, name="z_bf%d" % half, tag="z_bf%d" % half, align_bytes=64)
            staged = PACK - half
            for t in range(PACK):
                nc.scalar.activation(y_n1[:, t, :], y_win[t][:].indirect(n1_sb[:, entries]), COPY)
                nc.scalar.activation(y_n2[:, t, :], y_win[t][:].indirect(n2_sb[:, entries]), COPY)
                nc.vector.tensor_tensor(diff[:, t, :], y_n1[:, t, :], y_n2[:, t, :], ALU.subtract)
                nc.vector.scalar_tensor_tensor(
                    z[:, t, :] if t < staged else z_bf[:, :, t],
                    diff[:, t, :],
                    gs_sb[:, t : t + 1],
                    y_win[t][:, cols],
                    ALU.mult,
                    ALU.mult,
                )
                if t == staged - 1:
                    nc.vector.tensor_copy(
                        z_bf[:, :, :staged].rearrange("p (c i) t -> p c t i", i=4),
                        z[:].rearrange("p t (c i) -> p c t i", i=4),
                    )
            nc.vector.quantize_mx(
                out=z_codes[:, cols].bitcast(FP8X4),
                scales=z_scale[:, cols],
                in_=z_bf[:].rearrange("p c t -> p (c t)"),
            )
            second_product(0, cols)
            nc.scalar.activation(h_win[0][:, cols], h_ps[0][:, cols], COPY, scale=0.0625)

        nw = [keep.tile([P, S], F32, name="nw%d" % m) for m in range(H // P)]

        def product_out(m):
            second_product(m, slice(0, S))
            nc.vector.tensor_scalar(h_win[m][:, :S], h_ps[m][:], 0.0625, None, ALU.mult)

        def larger(m):
            h_n4 = keep.tile([P, S], F32, name="h_n4_%d" % m, tag="h_n4_%d" % m, align_bytes=64)
            nc.scalar.activation(h_n4[:], h_win[m][:].indirect(n4_sb[:]), COPY)
            nc.vector.tensor_tensor(nw[m][:], h_n4[:], h_win[m][:, :S], ALU.max)

        def put(m):
            page = pages[m % PAGES]
            nc.scalar.activation(page[:].indirect(n3_sb[:]), nw[m][:], COPY)
            nc.sync.dma_start(out[m * P : (m + 1) * P, :], page[:])

        product_out(1)
        pick_codewords("a", 1, "z_bf1")
        larger(0)
        pick_codewords("b", 1, "h_n4_0")
        larger(1)
        product_out(2)
        product_out(3)
        put(0)
        larger(2)
        put(1)
        larger(3)
        put(2)
        put(3)
